import numpy as np
import ml_dtypes

BF16 = ml_dtypes.bfloat16


def bf(x):
    return np.asarray(x, np.float32).astype(BF16)


def f32(x):
    return np.asarray(x, np.float32)


def f64(x):
    return np.asarray(x).astype(np.float64)


def striped(idx):
    return np.concatenate([l.reshape(-1, 16).T for l in idx])


def rows(idx, k):
    return np.tile(np.repeat(idx, 16, axis=0), (k // (16 * 8), 1))


def look(tab, idx):
    return np.take_along_axis(f64(tab), rows(idx, len(tab)), axis=1)


K, S, V, N, M = 512, 2048, 1536, 1536, 128


def setup_inputs():
    return {"tab": f32(np.random.standard_normal((K, S))), "y": f32(np.random.standard_normal((K, V))), "w": bf(np.random.standard_normal((K, M)) / np.sqrt(K)), "offs": striped(np.stack([np.random.permutation(S)[:N] for _ in range(8)]))}


def reference(tab, y, w, offs):
    idx = np.stack([g.T.reshape(-1) for g in np.split(offs, 8)])
    t = look(tab, idx)
    x = np.tanh(t) * f64(y)
    y = f64(w).T @ x
    return y

@@ -1,0 +1,54 @@
+import concourse.mybir as mybir
+
+BF16, F32, U16 = mybir.dt.bfloat16, mybir.dt.float32, mybir.dt.uint16
+TANH = mybir.ActivationFunctionType.Tanh
+MULT = mybir.AluOpType.mult
+
+P = 128
+K, S, N, M = 512, 2048, 1536, 128
+BLOCKS = K // P
+PIECE = 512
+PIECES = N // PIECE
+OFFS_PER_COLUMN = 16
+
+FLOPS = 2 * K * M * N
+
+
+def tile_lookup_gate_tanh_none_kernel(tc, tab, y, w, offs, out):
+    nc = tc.nc
+    with (
+        tc.tile_pool(name="held", bufs=1) as held,
+        tc.tile_pool(name="blocks", bufs=BLOCKS) as blocks,
+        tc.tile_pool(name="work", bufs=4) as work,
+        tc.psum_pool(name="psum", bufs=1) as psum,
+    ):
+        offsets = held.tile([P, N // OFFS_PER_COLUMN], U16)
+        nc.sync.dma_start(offsets[:], offs)
+
+        windows, streams = [], []
+        for b in range(BLOCKS):
+            window = blocks.tile([P, S], F32, name="window")
+            nc.sync.dma_start(window[:], tab[b * P : (b + 1) * P, :])
+            windows.append(window)
+            stream = blocks.tile([P, N], F32, name="stream")
+            nc.sync.dma_start(stream[:], y[b * P : (b + 1) * P, :])
+            streams.append(stream)
+            if b == 0:
+                weights = held.tile([P, BLOCKS, M], BF16)
+                nc.sync.dma_start(weights[:], w.rearrange("(b p) m -> p b m", p=P))
+
+        sums = [psum.tile([P, PIECE], F32, name=f"sums{i}") for i in range(PIECES)]
+        for b in range(BLOCKS):
+            for i in range(PIECES):
+                columns = slice(i * PIECE, (i + 1) * PIECE)
+                entries = slice(i * PIECE // OFFS_PER_COLUMN, (i + 1) * PIECE // OFFS_PER_COLUMN)
+                gate = work.tile([P, PIECE], F32, name="gate")
+                nc.scalar.activation(gate[:], windows[b][:].indirect(offsets[:, entries]), TANH)
+                x = work.tile([P, PIECE], BF16, name="x")
+                nc.vector.tensor_tensor(x[:], gate[:], streams[b][:, columns], MULT)
+                nc.tensor.matmul(sums[i][:], weights[:, b, :], x[:], start=b == 0, stop=b == BLOCKS - 1)
+
+        for i in range(PIECES):
+            result = work.tile([P, PIECE], F32, name="result")
+            nc.vector.tensor_copy(result[:], sums[i][:])
+            nc.sync.dma_start(out[:, i * PIECE : (i + 1) * PIECE], result[:])

@@ -25,16 +25,20 @@ def tile_lookup_gate_tanh_none_kernel(tc, tab, y, w, offs, out):
         offsets = held.tile([P, N // OFFS_PER_COLUMN], U16)
         nc.sync.dma_start(offsets[:], offs)
 
-        windows, streams = [], []
+        zero = held.tile([P, 1], F32)
+        nc.vector.memset(zero[:], 0.0)
+        unused = held.tile([P, 1], F32)
+        nc.scalar.activation(unused[:], zero[:], TANH)
+
+        windows = [blocks.tile([P, S], F32, name="window") for _ in range(BLOCKS)]
+        streams = [blocks.tile([P, N], F32, name="stream") for _ in range(BLOCKS)]
+        weights = held.tile([P, BLOCKS, M], BF16)
+        nc.sync.dma_start(windows[0][:], tab[0:P, :])
         for b in range(BLOCKS):
-            window = blocks.tile([P, S], F32, name="window")
-            nc.sync.dma_start(window[:], tab[b * P : (b + 1) * P, :])
-            windows.append(window)
-            stream = blocks.tile([P, N], F32, name="stream")
-            nc.sync.dma_start(stream[:], y[b * P : (b + 1) * P, :])
-            streams.append(stream)
+            if b + 1 < BLOCKS:
+                nc.sync.dma_start(windows[b + 1][:], tab[(b + 1) * P : (b + 2) * P, :])
+            nc.sync.dma_start(streams[b][:], y[b * P : (b + 1) * P, :])
             if b == 0:
-                weights = held.tile([P, BLOCKS, M], BF16)
                 nc.sync.dma_start(weights[:], w.rearrange("(b p) m -> p b m", p=P))
 
         sums = [psum.tile([P, PIECE], F32, name=f"sums{i}") for i in range(PIECES)]

@@ -8,7 +8,7 @@ P = 128
 K, S, N, M = 512, 2048, 1536, 128
 BLOCKS = K // P
 PIECE = 512
-PIECES = N // PIECE
+PARTS = ((0, 1), (2,))
 OFFS_PER_COLUMN = 16
 
 FLOPS = 2 * K * M * N
@@ -19,6 +19,7 @@ def tile_lookup_gate_tanh_none_kernel(tc, tab, y, w, offs, out):
     with (
         tc.tile_pool(name="held", bufs=1) as held,
         tc.tile_pool(name="blocks", bufs=BLOCKS) as blocks,
+        tc.tile_pool(name="gates", bufs=BLOCKS * len(PARTS[0])) as gates,
         tc.tile_pool(name="work", bufs=4) as work,
         tc.psum_pool(name="psum", bufs=1) as psum,
     ):
@@ -32,27 +33,37 @@ def tile_lookup_gate_tanh_none_kernel(tc, tab, y, w, offs, out):
 
         windows = [blocks.tile([P, S], F32, name="window") for _ in range(BLOCKS)]
         streams = [blocks.tile([P, N], F32, name="stream") for _ in range(BLOCKS)]
+        for b in range(BLOCKS):
+            nc.sync.dma_start(windows[b][:], tab[b * P : (b + 1) * P, :])
         weights = held.tile([P, BLOCKS, M], BF16)
-        nc.sync.dma_start(windows[0][:], tab[0:P, :])
-        for b in range(BLOCKS):
-            if b + 1 < BLOCKS:
-                nc.sync.dma_start(windows[b + 1][:], tab[(b + 1) * P : (b + 2) * P, :])
-            nc.sync.dma_start(streams[b][:], y[b * P : (b + 1) * P, :])
-            if b == 0:
-                nc.sync.dma_start(weights[:], w.rearrange("(b p) m -> p b m", p=P))
+        nc.sync.dma_start(weights[:], w.rearrange("(b p) m -> p b m", p=P))
+        for part in PARTS:
+            columns = slice(part[0] * PIECE, (part[-1] + 1) * PIECE)
+            for b in range(BLOCKS):
+                nc.sync.dma_start(streams[b][:, columns], y[b * P : (b + 1) * P, columns])
 
-        sums = [psum.tile([P, PIECE], F32, name=f"sums{i}") for i in range(PIECES)]
-        for b in range(BLOCKS):
-            for i in range(PIECES):
-                columns = slice(i * PIECE, (i + 1) * PIECE)
-                entries = slice(i * PIECE // OFFS_PER_COLUMN, (i + 1) * PIECE // OFFS_PER_COLUMN)
-                gate = work.tile([P, PIECE], F32, name="gate")
-                nc.scalar.activation(gate[:], windows[b][:].indirect(offsets[:, entries]), TANH)
-                x = work.tile([P, PIECE], BF16, name="x")
-                nc.vector.tensor_tensor(x[:], gate[:], streams[b][:, columns], MULT)
-                nc.tensor.matmul(sums[i][:], weights[:, b, :], x[:], start=b == 0, stop=b == BLOCKS - 1)
+        gate = {}
+        for part in PARTS:
+            for b in range(BLOCKS):
+                for i in part:
+                    entries = slice(i * PIECE // OFFS_PER_COLUMN, (i + 1) * PIECE // OFFS_PER_COLUMN)
+                    gate[b, i] = gates.tile([P, PIECE], F32, name="gate")
+                    nc.scalar.activation(gate[b, i][:], windows[b][:].indirect(offsets[:, entries]), TANH)
 
-        for i in range(PIECES):
-            result = work.tile([P, PIECE], F32, name="result")
-            nc.vector.tensor_copy(result[:], sums[i][:])
-            nc.sync.dma_start(out[:, i * PIECE : (i + 1) * PIECE], result[:])
+        half = PIECE // 2
+        chunks = {0: [(0, PIECE)], 1: [(0, PIECE)], 2: [(0, half), (half, half)]}
+        sums = {(i, c): psum.tile([P, width], F32, name=f"sums{i}_{c}") for i in chunks for c, width in chunks[i]}
+        for part in PARTS:
+            for b in range(BLOCKS):
+                for i in part:
+                    x = work.tile([P, PIECE], BF16, name="x")
+                    nc.vector.tensor_tensor(x[:], gate[b, i][:], streams[b][:, i * PIECE : (i + 1) * PIECE], MULT)
+                    for c, width in chunks[i]:
+                        nc.tensor.matmul(
+                            sums[i, c][:], weights[:, b, :], x[:, c : c + width], start=b == 0, stop=b == BLOCKS - 1
+                        )
+            finished = [(i, c, width) for i in part for c, width in chunks[i]]
+            for copy, (i, c, width) in zip((nc.vector.tensor_copy, nc.scalar.copy), finished):
+                result = work.tile([P, width], F32, name=f"result{width}")
+                copy(result[:], sums[i, c][:])
+                nc.sync.dma_start(out[:, i * PIECE + c : i * PIECE + c + width], result[:])

import concourse.mybir as mybir

BF16, F32, U16 = mybir.dt.bfloat16, mybir.dt.float32, mybir.dt.uint16
TANH = mybir.ActivationFunctionType.Tanh
MULT = mybir.AluOpType.mult

P = 128
K, S, N, M = 512, 2048, 1536, 128
BLOCKS = K // P
PIECE = 512
PARTS = ((0, 1), (2,))
OFFS_PER_COLUMN = 16

FLOPS = 2 * K * M * N


def tile_lookup_gate_tanh_none_kernel(tc, tab, y, w, offs, out):
    nc = tc.nc
    with (
        tc.tile_pool(name="held", bufs=1) as held,
        tc.tile_pool(name="blocks", bufs=BLOCKS) as blocks,
        tc.tile_pool(name="gates", bufs=BLOCKS * len(PARTS[0])) as gates,
        tc.tile_pool(name="work", bufs=4) as work,
        tc.psum_pool(name="psum", bufs=1) as psum,
    ):
        offsets = held.tile([P, N // OFFS_PER_COLUMN], U16)
        nc.sync.dma_start(offsets[:], offs)

        zero = held.tile([P, 1], F32)
        nc.vector.memset(zero[:], 0.0)
        unused = held.tile([P, 1], F32)
        nc.scalar.activation(unused[:], zero[:], TANH)

        windows = [blocks.tile([P, S], F32, name="window") for _ in range(BLOCKS)]
        streams = [blocks.tile([P, N], F32, name="stream") for _ in range(BLOCKS)]
        for b in range(BLOCKS):
            nc.sync.dma_start(windows[b][:], tab[b * P : (b + 1) * P, :])
        weights = held.tile([P, BLOCKS, M], BF16)
        nc.sync.dma_start(weights[:], w.rearrange("(b p) m -> p b m", p=P))
        for part in PARTS:
            columns = slice(part[0] * PIECE, (part[-1] + 1) * PIECE)
            for b in range(BLOCKS):
                nc.sync.dma_start(streams[b][:, columns], y[b * P : (b + 1) * P, columns])

        gate = {}
        for part in PARTS:
            for b in range(BLOCKS):
                for i in part:
                    entries = slice(i * PIECE // OFFS_PER_COLUMN, (i + 1) * PIECE // OFFS_PER_COLUMN)
                    gate[b, i] = gates.tile([P, PIECE], F32, name="gate")
                    nc.scalar.activation(gate[b, i][:], windows[b][:].indirect(offsets[:, entries]), TANH)

        half = PIECE // 2
        chunks = {0: [(0, PIECE)], 1: [(0, PIECE)], 2: [(0, half), (half, half)]}
        sums = {(i, c): psum.tile([P, width], F32, name=f"sums{i}_{c}") for i in chunks for c, width in chunks[i]}
        for part in PARTS:
            for b in range(BLOCKS):
                for i in part:
                    x = work.tile([P, PIECE], BF16, name="x")
                    nc.vector.tensor_tensor(x[:], gate[b, i][:], streams[b][:, i * PIECE : (i + 1) * PIECE], MULT)
                    for c, width in chunks[i]:
                        nc.tensor.matmul(
                            sums[i, c][:], weights[:, b, :], x[:, c : c + width], start=b == 0, stop=b == BLOCKS - 1
                        )
            finished = [(i, c, width) for i in part for c, width in chunks[i]]
            for copy, (i, c, width) in zip((nc.vector.tensor_copy, nc.scalar.copy), finished):
                result = work.tile([P, width], F32, name=f"result{width}")
                copy(result[:], sums[i, c][:])
                nc.sync.dma_start(out[:, i * PIECE + c : i * PIECE + c + width], result[:])
